import numpy as np
CORES = [112,113,114,115,124,125,126,127]
N = 8
def setup_inputs(rng):
    return {"x1": rng.standard_normal((N, 128, 64), dtype=np.float32), "x2": rng.standard_normal((N, 128, 1), dtype=np.float32), "x3": rng.standard_normal((N, 128, 256), dtype=np.float32), "x4": rng.standard_normal((N, 128, 16), dtype=np.float32)}
def reference(x1, x2, x3, x4):
    out = {}
    s = x1.sum(axis=0, dtype=np.float64).astype(x1.dtype)
    out["y1"] = np.broadcast_to(s, (N,) + s.shape)
    s = x2.sum(axis=0, dtype=np.float64).astype(x2.dtype)
    out["y2"] = np.broadcast_to(s, (N,) + s.shape)
    s = x3.sum(axis=0, dtype=np.float64).astype(x3.dtype)
    out["y3"] = np.broadcast_to(s, (N,) + s.shape)
    s = x4.sum(axis=0, dtype=np.float64).astype(x4.dtype)
    out["y4"] = np.broadcast_to(s, (N,) + s.shape)
    return out

from concourse.bass import DstId, RemoteDMATransfer

F32 = "float32"
SCRATCH = {
    "ps": ("dram", [128, 64], F32), "pm": ("dram", [128, 17], F32),
    "pa": ("dram", [128, 88], F32), "pb": ("dram", [2, 128, 84], F32),
    "ls": ("dram", [5, 128, 64], F32), "lm": ("dram", [5, 128, 17], F32), "la": ("dram", [5, 128, 88], F32),
    "lb": ("dram", [4, 128, 84], F32),
    "fb": ("dram", [2, 128, 84], F32),
    "rs": ("dram", [128, 64], F32), "rm": ("dram", [128, 17], F32),
    "ra": ("dram", [128, 88], F32), "rb": ("dram", [2, 128, 84], F32),
}
SEMAPHORES = ["ld_s", "ld_m", "ld_a", "ld_b", "arr_s", "arr_m", "arr_a", "arr_b",
              "part_s", "part_m", "part_a", "part_b", "tot_s", "tot_m", "tot_a", "tot_b", "sent", "st"]

ON_CHIP = 0xFFFF
OFF_CHIP = 0x00FF
UPPER = 0xFF00


def chip_plan(T, topo):
    chips = sorted(set(topo.chip(c) for c in T.cores))
    out = {}
    for ch in chips:
        mate = [o for o in chips if o != ch][0]
        cores = [ch * 8 + k for k in range(8)]
        ranks = [c for c in cores if c in T.cores]
        gates = [c for c in cores if topo.may_write(c, mate * 8)]
        out[ch] = {
            "mate": mate,
            "ranks": ranks,
            "hgate": [c for c in gates if c not in ranks],
            "rgate": [c for c in gates if c in ranks],
            "plain": [c for c in cores if c not in ranks and c not in gates],
        }
    return out


def rank_program(g, core, T, topo):
    plan = chip_plan(T, topo)
    if topo.chip(core) not in plan:
        return
    near = plan[topo.chip(core)]
    far = plan[near["mate"]]
    ranks = near["ranks"]
    sem = T.sem
    sent = [0]

    def dst_id(c):
        rid, pid, ring = topo.addr(c)
        return DstId(rid=rid, pnc=pid)

    def call(transfers):
        g.remote_dma_fused(
            [RemoteDMATransfer(dst_ids=[dst_id(c) for c, ap in dsts], dma_engine_mask=mask, remote_sem=rsem,
                               srcs=srcs, dsts=[ap for c, ap in dsts], alu_op=1 if len(srcs) > 1 else 0)
             for srcs, dsts, mask, rsem in transfers],
            local_sem=sem.sent)
        for srcs, dsts, mask, rsem in transfers:
            sent[0] += bin(mask).count("1")

    if core in near["hgate"]:
        k = near["hgate"].index(core)
        names = ("s", "m") if k == 0 else ("a",)
        twin = far["hgate"][k]
        for n in names:
            land = T["l" + n]
            g.wait_ge(sem["arr_" + n], 4 * 16)
            call([([land[j] for j in range(4)], [(twin, land[4])], OFF_CHIP, sem["part_" + n])])
        for n in names:
            land = T["l" + n]
            g.wait_ge(sem["part_" + n], 8)
            call([([land[j] for j in range(5)], [(c, T["r" + n][:]) for c in ranks], ON_CHIP, sem["tot_" + n])])
        g.wait_ge(sem.sent, sent[0])
        return

    if core in near["plain"]:
        k = near["plain"].index(core)
        g.wait_ge(sem.part_b, 8 + 8)
        call([([T.fb[0], T.fb[1]], [(c, T.rb[k]) for c in ranks], ON_CHIP, sem.tot_b)])
        g.wait_ge(sem.sent, sent[0])
        return

    me = ranks.index(core)
    sy, sc = g.sync, g.scalar

    sy.dma_start(T.pb[:], T.x3[44:128, :]).then_inc(sem.ld_b, 16)
    sc.dma_start(T.pa[:], T.x3[0:44, :]).then_inc(sem.ld_a, 16)
    sc.dma_start(T.ps[34:128, :], T.x1[0:94, :]).then_inc(sem.ld_s, 16)
    sy.dma_start(T.ps[0:32, :], T.x4[:]).then_inc(sem.ld_s, 16)
    sy.dma_start(T.ps[32:34, :], T.x2[:]).then_inc(sem.ld_s, 16)
    sc.dma_start(T.pm[:], T.x1[94:128, :]).then_inc(sem.ld_m, 16)

    g.wait_ge(sem.ld_a, 16)
    call([([T.pa[:]], [(near["hgate"][1], T.la[me])], ON_CHIP, sem.arr_a)])
    g.wait_ge(sem.ld_b, 16)
    to = [k for k in range(2) if near["rgate"][k] != core]
    masks = (ON_CHIP,) if len(to) == 1 else (OFF_CHIP, UPPER)
    call([([T.pb[k]], [(near["rgate"][k], T.lb[me])], masks[i], sem.arr_b) for i, k in enumerate(to)])
    g.wait_ge(sem.ld_s, 3 * 16)
    call([([T.ps[:]], [(near["hgate"][0], T.ls[me])], ON_CHIP, sem.arr_s)])
    g.wait_ge(sem.ld_m, 16)
    call([([T.pm[:]], [(near["hgate"][0], T.lm[me])], ON_CHIP, sem.arr_m)])

    if core in near["rgate"]:
        k = near["rgate"].index(core)
        g.wait_ge(sem.arr_b, 8 + 8 + 16)
        srcs = [T.pb[k]] + [T.lb[j] for j in range(4) if j != me]
        call([(srcs, [(far["plain"][k], T.fb[1])], OFF_CHIP, sem.part_b),
              (srcs, [(near["plain"][k], T.fb[0])], UPPER, sem.part_b)])

    sy.wait_ge(sem.tot_b, 2 * 16)
    sy.dma_start(T.y3[44:128, :], T.rb[:]).then_inc(sem.st, 16)
    sc.wait_ge(sem.tot_a, 16)
    sc.dma_start(T.y3[0:44, :], T.ra[:]).then_inc(sem.st, 16)
    sc.wait_ge(sem.tot_s, 16)
    sc.dma_start(T.y1[0:94, :], T.rs[34:128, :]).then_inc(sem.st, 16)
    sy.wait_ge(sem.tot_s, 16)
    sy.dma_start(T.y4[:], T.rs[0:32, :]).then_inc(sem.st, 16)
    sy.dma_start(T.y2[:], T.rs[32:34, :]).then_inc(sem.st, 16)
    sc.wait_ge(sem.tot_m, 16)
    sc.dma_start(T.y1[94:128, :], T.rm[:]).then_inc(sem.st, 16)

    g.wait_ge(sem.sent, sent[0])
    g.wait_ge(sem.st, 6 * 16)
